import numpy as np
import ml_dtypes


def mxq(x, axis, fmt="e4m3"):
    dtype, down = {"e4m3": (ml_dtypes.float8_e4m3fn, 7), "e5m2": (ml_dtypes.float8_e5m2, 14)}[fmt]
    v = np.moveaxis(np.asarray(x, np.float32).astype(ml_dtypes.bfloat16).astype(np.float64), axis, -1)
    blocks = v.reshape(v.shape[:-1] + (-1, 32))
    amax = np.abs(blocks).max(-1, keepdims=True)
    byte = np.maximum(np.where(amax > 0, np.frexp(amax)[1] - 1 + 127, 0) - down, 1)
    scale = np.exp2(byte - 127.0)
    codes = (blocks / scale).astype(np.float32).astype(dtype).astype(np.float64)
    return np.moveaxis((codes * scale).reshape(v.shape), -1, axis)


WIDE = False


def mx_kscale(k):
    if not WIDE:
        return np.ones(k)
    levels = np.array([10, -10, 5, -5, 0])
    if k % 512:
        return np.exp2(np.random.permutation(np.resize(levels, k // 32))).repeat(32)
    a = np.empty((k // 512, 16))
    for p in range(k // 512):
        a[p, :8] = np.random.permutation(np.resize(levels, 8))
        for g in range(8):
            far = levels[np.abs(levels - a[p, g]) >= 10]
            a[p, g + 8] = far[np.random.randint(len(far))]
    return np.exp2(a.ravel()).repeat(32)


BF16 = ml_dtypes.bfloat16


def bf(x):
    return np.asarray(x, np.float32).astype(BF16)


def f64(x):
    return np.asarray(x).astype(np.float64)


E2M1 = np.array([0.0, 0.5, 1.0, 1.5, 2.0, 3.0, 4.0, 6.0, -0.0, -0.5, -1.0, -1.5, -2.0, -3.0, -4.0, -6.0])


def pack_weight(w, fmt):
    k, n = w.shape
    w = f64(bf(w)).reshape(k // 32, 32, n)
    amax = np.abs(w).max(1)
    if fmt == "e4m3":
        byte = np.frexp(amax)[1] - 1 + 127 - 7
    else:
        mant, ex = np.frexp(amax / 6.0)
        byte = np.where(mant > 0.5, ex, ex - 1) + 127
    byte = np.clip(np.where(amax > 0, byte, 1), 1, 254)
    scaled = (w * np.exp2(127.0 - byte)[:, None, :]).reshape(k, n).astype(np.float32)
    by_word = np.ascontiguousarray(scaled.reshape(k // 512, 128, 4, n).transpose(0, 1, 3, 2))
    if fmt == "e4m3":
        words = by_word.astype(ml_dtypes.float8_e4m3fn).view(np.uint8)
    else:
        c = by_word.astype(ml_dtypes.float4_e2m1fn).view(np.uint8) & 0xF
        words = c[..., 0::2] | (c[..., 1::2] << 4)
    return np.ascontiguousarray(words), np.ascontiguousarray(byte.astype(np.uint8).reshape(k // 512, 16, n))


def unpack_weight(words, scales, fmt):
    g, p, n, _ = words.shape
    if fmt == "e4m3":
        vals = np.ascontiguousarray(words).view(ml_dtypes.float8_e4m3fn).astype(np.float64)
    else:
        nib = np.empty((g, p, n, 4), np.uint8)
        nib[..., 0::2] = words & 0xF
        nib[..., 1::2] = words >> 4
        vals = E2M1[nib]
    vals = vals * np.repeat(np.exp2(scales.astype(np.float64) - 127.0), 8, axis=1)[..., None]
    return vals.transpose(0, 1, 3, 2).reshape(g * 512, n)
def pack4(w):
    words, scales = pack_weight(w, "e2m1")
    return words.reshape(words.shape[0], 128, -1), scales


def unpack4(words, scales):
    return unpack_weight(words.reshape(words.shape[0], 128, -1, 2), scales, "e2m1")


T, K, N = 512, 1536, 1536


def setup_inputs():
    s = mx_kscale(K)
    dipoles = bf(np.random.standard_normal((T, K)) * s)
    w_ref = np.random.standard_normal((K, N)) / np.sqrt(K) / s[:, None]
    w_site = np.random.standard_normal((K, N)) / np.sqrt(K) / s[:, None]
    w_breath = bf(np.random.standard_normal((K, N)) / np.sqrt(K) / s[:, None])
    ref_words, ref_scales = pack4(w_ref)
    site_words, site_scales = pack_weight(w_site, "e4m3")
    return {"dipoles": dipoles,
            "ref_words": ref_words, "ref_scales": ref_scales,
            "site_words": site_words, "site_scales": site_scales,
            "w_breath": w_breath,
            "resp": bf(np.random.standard_normal(T)),
            "gain": bf(1 + 0.1 * np.random.standard_normal(N))}


def reference(dipoles, ref_words, ref_scales, site_words, site_scales, w_breath, resp, gain):
    d = mxq(f64(dipoles), 1, "e4m3")
    v_ref = d @ unpack4(ref_words, ref_scales)
    v_site = d @ unpack_weight(site_words, site_scales, "e4m3")
    v_breath = d @ mxq(f64(w_breath), 0, "e4m3")
    lead = v_site - v_ref + f64(resp)[:, None] * v_breath
    return lead * f64(gain)

@@ -1,0 +1,350 @@
+from contextlib import ExitStack
+
+import concourse.mybir as mybir
+from concourse.masks import make_identity
+
+T, K, N = 512, 1536, 1536
+FLOPS = 3 * 2 * T * K * N
+
+F32 = mybir.dt.float32
+BF16 = mybir.dt.bfloat16
+I32 = mybir.dt.int32
+U32 = mybir.dt.uint32
+U8 = mybir.dt.uint8
+FP8X4 = mybir.dt.float8_e4m3fn_x4
+FP4X4 = mybir.dt.float4_e2m1fn_x4
+ALU = mybir.AluOpType
+
+P = 128
+PACK = 4
+K_PASS = P * PACK
+PASSES = K // K_PASS
+TILES = T // P
+BANK = 512
+CHUNKS = N // BANK
+UNITS = TILES * PASSES
+SITE_ROW = 4
+SCALAR_COLS = 320
+LEAD = (4, 4, 2)
+
+
+def tile_twelve_lead_ecg_synthesis_s10_kernel(
+    tc, dipoles, ref_words, ref_scales, site_words, site_scales, w_breath, resp, gain, out
+):
+    nc = tc.nc
+    with ExitStack() as ctx:
+        sb = ctx.enter_context(tc.tile_pool(name="sb", bufs=1))
+        ps = ctx.enter_context(tc.psum_pool(name="ps", bufs=1))
+        ctx.enter_context(tc.manual_schedule())
+
+        def sbuf(name, shape, dtype):
+            return sb.tile(shape, dtype, name=name, align_bytes=64)
+
+        a_banks = [ps.tile([P, BANK], F32, name="a_bank%d" % i) for i in range(TILES)]
+        b_banks = [ps.tile([P, BANK], F32, name="b_bank%d" % i) for i in range(TILES)]
+
+        ident = sbuf("ident", [P, P], F32)
+        gain_col = sbuf("gain_col", [P, CHUNKS * PACK], BF16)
+        gain_all = sbuf("gain_all", [P, N], BF16)
+        resp_col = sbuf("resp_col", [P, TILES], BF16)
+        d_rows = [sbuf("d_rows%d" % i, [P, K], BF16) for i in range(TILES)]
+        d_pos = sbuf("d_pos", [P, UNITS * K_PASS], BF16)
+        d_neg = sbuf("d_neg", [P, UNITS * K_PASS], BF16)
+        pos_codes = sbuf("pos_codes", [P, UNITS * P], U32)
+        pos_scales = sbuf("pos_scales", [P, UNITS * P], U8)
+        neg_codes = sbuf("neg_codes", [P, UNITS * P], U32)
+        neg_scales = sbuf("neg_scales", [P, UNITS * P], U8)
+        ref_codes = [sbuf("ref_codes%d" % c, [P, PASSES, 2 * BANK], U8) for c in range(CHUNKS)]
+        site_first = [sbuf("site_first%d" % g, [P, BANK], U32) for g in range(PASSES)]
+        site_later = [sbuf("site_later%d" % c, [P, PASSES, BANK], U32) for c in range(1, CHUNKS)]
+        widths = (BANK, N - BANK)
+        ref_planes = [sbuf("ref_plane%d" % s, [P, PASSES, w], U8) for s, w in enumerate(widths)]
+        site_planes = [sbuf("site_plane%d" % s, [P, PASSES, w], U8) for s, w in enumerate(widths)]
+        cg = [(c, g) for c in range(CHUNKS) for g in range(PASSES)]
+        w_rows = {k: sbuf("w_rows%d_%d" % k, [P, PACK, BANK], BF16) for k in cg}
+        w_quads = {k: sbuf("w_quads%d_%d" % k, [P, PACK * BANK], BF16) for k in cg}
+        w_codes = {k: sbuf("w_codes%d_%d" % k, [P, BANK], U32) for k in cg}
+        w_scales = {k: sbuf("w_scales%d_%d" % k, [P, BANK], U8) for k in cg}
+        result = {(c, i): sbuf("result%d_%d" % (c, i), [P, BANK], F32) for c in range(CHUNKS) for i in range(TILES)}
+
+        d_hbm = dipoles.rearrange("(p i) k -> i p k", i=TILES)
+        out_hbm = out.rearrange("(p i) n -> i p n", i=TILES)
+        ref_hbm = ref_words.bitcast(I32)
+        site_hbm = site_words.rearrange("g p n t -> g p (n t)").bitcast(I32)
+
+        def zero_plane(engine, plane):
+            engine.memset(plane[:].rearrange("p g n -> p (g n)").bitcast(I32), 0)
+
+        def load_plane(queue, plane, scales, row, s):
+            words = scales.bitcast(I32)
+            n0 = 0 if s == 0 else BANK // 4
+            for q in range(4):
+                queue.dma_start(
+                    out=plane[32 * q + row : 32 * q + row + 4, :, :].bitcast(I32),
+                    in_=words[:, 4 * q : 4 * q + 4, n0 : n0 + widths[s] // 4].rearrange("g r n -> r g n"),
+                )
+
+        def load_ref(c):
+            nc.sync.dma_start(
+                out=ref_codes[c][:].bitcast(I32),
+                in_=ref_hbm[:, :, c * BANK // 2 : (c + 1) * BANK // 2].rearrange("g p w -> p g w"),
+            )
+
+        def load_site(c):
+            cols = slice(c * BANK, (c + 1) * BANK)
+            if c == 0:
+                for g in range(PASSES):
+                    nc.sync.dma_start(out=site_first[g][:].bitcast(I32), in_=site_hbm[g, :, cols])
+            else:
+                nc.sync.dma_start(
+                    out=site_later[c - 1][:].bitcast(I32), in_=site_hbm[:, :, cols].rearrange("g p n -> p g n")
+                )
+
+        def load_breath(c):
+            for g in range(PASSES):
+                rows = w_breath[g * K_PASS : (g + 1) * K_PASS, c * BANK : (c + 1) * BANK]
+                nc.sync.dma_start(out=w_rows[c, g][:], in_=rows.rearrange("(p j) n -> p j n", j=PACK))
+
+        nc.scalar.dma_start(
+            out=gain_col[:].rearrange("p (c j) -> p c j", j=PACK),
+            in_=gain.rearrange("(c p j) -> p c j", p=P, j=PACK),
+        )
+        nc.scalar.dma_start(out=resp_col[:], in_=resp.rearrange("(p i) -> p i", i=TILES))
+        zero_plane(nc.vector, ref_planes[0])
+        make_identity(nc, ident[:])
+        zero_plane(nc.gpsimd, site_planes[0])
+        zero_plane(nc.vector, ref_planes[1])
+        zero_plane(nc.vector, site_planes[1])
+        load_plane(nc.gpsimd, site_planes[0], site_scales, SITE_ROW, 0)
+        for i in range(TILES):
+            nc.sync.dma_start(out=d_rows[i][:], in_=d_hbm[i])
+        load_plane(nc.sync, ref_planes[0], ref_scales, 0, 0)
+        load_ref(0)
+        load_site(0)
+        load_breath(0)
+        load_plane(nc.sync, ref_planes[1], ref_scales, 0, 1)
+        load_ref(1)
+        load_site(1)
+        load_plane(nc.sync, site_planes[1], site_scales, SITE_ROW, 1)
+        load_breath(1)
+        load_breath(2)
+        load_ref(2)
+        load_site(2)
+
+        gain_words = gain_col[:].bitcast(F32)
+        for w in range(2 * CHUNKS):
+            nc.tensor.transpose(
+                a_banks[w // 4][:, (w % 4) * P : (w % 4 + 1) * P],
+                gain_words[:, w : w + 1].to_broadcast([P, P]),
+                ident[:],
+            )
+        for b, count in enumerate((2, 1)):
+            nc.vector.tensor_copy(
+                out=gain_all[:, 2 * b * BANK : (2 * b + count) * BANK]
+                .bitcast(F32)
+                .rearrange("p (c r h) -> p c r h", c=count, h=2),
+                in_=a_banks[b][:, : count * 2 * P].rearrange("p (c h r) -> p c r h", c=count, h=2),
+            )
+
+        t_banks = b_banks + a_banks[2:]
+
+        def turn(j):
+            for u in (2 * j, 2 * j + 1):
+                i, g = divmod(u, PASSES)
+                words = d_rows[i][:].bitcast(F32)
+                for h in range(2):
+                    slot = 2 * (u % 2) + h
+                    nc.tensor.transpose(
+                        t_banks[j][:, slot * P : (slot + 1) * P],
+                        words[:, 2 * P * g + h : 2 * P * (g + 1) : 2],
+                        ident[:],
+                    )
+            nc.scalar.copy(
+                out=d_pos[:, 2 * j * K_PASS : 2 * (j + 1) * K_PASS]
+                .bitcast(F32)
+                .rearrange("p (u r h) -> p u r h", u=2, h=2),
+                in_=t_banks[j][:].rearrange("p (u h r) -> p u r h", u=2, h=2),
+            )
+
+        def quantize(values, codes, scales, u0, u1):
+            nc.vector.quantize_mx(
+                out=codes[:, u0 * P : u1 * P].bitcast(FP8X4),
+                scales=scales[:, u0 * P : u1 * P],
+                in_=values[:, u0 * K_PASS : u1 * K_PASS],
+            )
+
+        def quantize_pos(j):
+            quantize(d_pos, pos_codes, pos_scales, 2 * j, 2 * j + 2)
+
+        def negate(m):
+            cols = slice(4 * m * K_PASS, 4 * (m + 1) * K_PASS)
+            nc.vector.tensor_scalar_mul(out=d_neg[:, cols], in0=d_pos[:, cols], scalar1=-1.0)
+
+        def quantize_neg(m):
+            quantize(d_neg, neg_codes, neg_scales, 4 * m, 4 * m + 4)
+
+        def interleave(copy, c, g, n0, n1):
+            copy(
+                out=w_quads[c, g][:, PACK * n0 : PACK * n1].rearrange("p (m i t) -> p m t i", i=4, t=PACK),
+                in_=w_rows[c, g][:, :, n0:n1].rearrange("p t (m i) -> p m t i", i=4),
+            )
+
+        def interleave_scalar(c, g):
+            interleave(nc.scalar.copy, c, g, 0, SCALAR_COLS)
+
+        def interleave_vector(c, g):
+            interleave(nc.vector.tensor_copy, c, g, SCALAR_COLS, BANK)
+
+        def quantize_breath(c, g):
+            nc.vector.quantize_mx(out=w_codes[c, g][:].bitcast(FP8X4), scales=w_scales[c, g][:], in_=w_quads[c, g][:])
+
+        def plane_cols(c):
+            s = min(c, 1)
+            return s, slice((c - s) * BANK, (c - s + 1) * BANK)
+
+        def mm_ref(c, i):
+            s, cols = plane_cols(c)
+            for g in range(PASSES):
+                u = slice((PASSES * i + g) * P, (PASSES * i + g + 1) * P)
+                nc.tensor.matmul_mx(
+                    out=a_banks[i][:],
+                    lhsT=pos_codes[:, u].bitcast(FP8X4),
+                    lhsT_scale=pos_scales[:, u],
+                    rhs=ref_codes[c][:, g, :].bitcast(FP4X4),
+                    rhs_scale=ref_planes[s][:, g, cols],
+                    start=(g == 0),
+                    stop=False,
+                )
+
+        def mm_site(c, i):
+            s, cols = plane_cols(c)
+            for g in range(PASSES):
+                u = slice((PASSES * i + g) * P, (PASSES * i + g + 1) * P)
+                codes = site_first[g][:] if c == 0 else site_later[c - 1][:, g, :]
+                nc.tensor.matmul_mx(
+                    out=a_banks[i][:],
+                    lhsT=neg_codes[:, u].bitcast(FP8X4),
+                    lhsT_scale=neg_scales[:, u],
+                    rhs=codes.bitcast(FP8X4),
+                    rhs_scale=site_planes[s][SITE_ROW:, g, cols],
+                    start=False,
+                    stop=(g == PASSES - 1),
+                )
+
+        def mm_breath(c, i, bank, cols):
+            for g in range(PASSES):
+                u = slice((PASSES * i + g) * P, (PASSES * i + g + 1) * P)
+                nc.tensor.matmul_mx(
+                    out=bank[:, cols],
+                    lhsT=pos_codes[:, u].bitcast(FP8X4),
+                    lhsT_scale=pos_scales[:, u],
+                    rhs=w_codes[c, g][:, cols].bitcast(FP8X4),
+                    rhs_scale=w_scales[c, g][:, cols],
+                    start=(g == 0),
+                    stop=(g == PASSES - 1),
+                )
+
+        whole = slice(0, BANK)
+
+        def park(c, i):
+            nc.scalar.copy(out=result[c, i][:], in_=a_banks[i][:])
+
+        def combine(c, i, bank, cols):
+            nc.vector.scalar_tensor_tensor(
+                out=result[c, i][:, cols],
+                in0=bank[:, cols],
+                scalar=resp_col[:, i : i + 1],
+                in1=result[c, i][:, cols],
+                op0=ALU.mult,
+                op1=ALU.subtract,
+            )
+
+        def finish(c, i, cols):
+            n = slice(c * BANK + cols.start, c * BANK + cols.stop)
+            nc.vector.tensor_tensor(
+                out=result[c, i][:, cols], in0=result[c, i][:, cols], in1=gain_all[:, n], op=ALU.mult
+            )
+            nc.sync.dma_start(out=out_hbm[i][:, n], in_=result[c, i][:, cols])
+
+        for j in range(UNITS // 2):
+            turn(j)
+            quantize_pos(j)
+            if j % 2 == 1:
+                negate(j // 2)
+            elif j > 0:
+                quantize_neg(j // 2 - 1)
+
+        for g in range(PASSES):
+            interleave_scalar(0, g)
+        interleave_vector(0, 0)
+        quantize_neg(2)
+        interleave_vector(0, 1)
+        quantize_breath(0, 0)
+        interleave_vector(0, 2)
+        quantize_breath(0, 1)
+        quantize_breath(0, 2)
+        for i in range(TILES):
+            mm_ref(0, i)
+        for i in range(TILES):
+            mm_site(0, i)
+            park(0, i)
+        for i in range(TILES):
+            mm_breath(0, i, b_banks[i], whole)
+            combine(0, i, b_banks[i], whole)
+            if i > 0:
+                finish(0, i - 1, whole)
+
+        for g in range(PASSES):
+            interleave_scalar(1, g)
+        interleave_vector(1, 0)
+        finish(0, TILES - 1, whole)
+        interleave_vector(1, 1)
+        quantize_breath(1, 0)
+        interleave_vector(1, 2)
+        quantize_breath(1, 1)
+        interleave_vector(2, 0)
+        quantize_breath(1, 2)
+        interleave_vector(2, 1)
+        interleave_vector(2, 2)
+        for i in range(TILES):
+            mm_ref(1, i)
+            mm_site(1, i)
+            park(1, i)
+            if i == 1:
+                interleave_scalar(2, 0)
+        interleave_scalar(2, 1)
+        interleave_scalar(2, 2)
+        quantize_breath(2, 0)
+        for i in range(TILES):
+            mm_breath(1, i, b_banks[i], whole)
+            combine(1, i, b_banks[i], whole)
+            if i > 0:
+                finish(1, i - 1, whole)
+        quantize_breath(2, 1)
+        finish(1, TILES - 1, whole)
+        quantize_breath(2, 2)
+
+        for i in range(2):
+            mm_ref(2, i)
+            mm_site(2, i)
+            park(2, i)
+        for i in range(2):
+            mm_breath(2, i, b_banks[i], whole)
+            combine(2, i, b_banks[i], whole)
+        for i in range(2):
+            finish(2, i, whole)
+        mm_ref(2, 2)
+        mm_site(2, 2)
+        park(2, 2)
+        mm_breath(2, 2, b_banks[2], whole)
+        combine(2, 2, b_banks[2], whole)
+        finish(2, 2, whole)
+        mm_ref(2, 3)
+        mm_site(2, 3)
+        park(2, 3)
+        halves = ((b_banks[3], slice(0, BANK // 2)), (a_banks[0], slice(BANK // 2, BANK)))
+        for bank, cols in halves:
+            mm_breath(2, 3, bank, cols)
+            combine(2, 3, bank, cols)
+        for bank, cols in halves:
+            finish(2, 3, cols)

@@ -24,8 +24,8 @@ BANK = 512
 CHUNKS = N // BANK
 UNITS = TILES * PASSES
 SITE_ROW = 4
-SCALAR_COLS = 320
-LEAD = (4, 4, 2)
+SCALAR_COLS = (192, 320, 384)
+GAIN_WORDS = N // P // 2
 
 
 def tile_twelve_lead_ecg_synthesis_s10_kernel(
@@ -40,14 +40,21 @@ def tile_twelve_lead_ecg_synthesis_s10_kernel(
         def sbuf(name, shape, dtype):
             return sb.tile(shape, dtype, name=name, align_bytes=64)
 
-        a_banks = [ps.tile([P, BANK], F32, name="a_bank%d" % i) for i in range(TILES)]
-        b_banks = [ps.tile([P, BANK], F32, name="b_bank%d" % i) for i in range(TILES)]
+        banks = [ps.tile([P, BANK], F32, name="bank%d" % b) for b in range(8)]
+        groups = (
+            [("a", 0, i) for i in range(TILES)] + [("b", 0, i) for i in range(TILES)]
+            + [("a", 1, i) for i in range(TILES)] + [("b", 1, i) for i in range(TILES)]
+            + [("a", 2, i) for i in range(3)] + [("b", 2, i) for i in range(3)]
+            + [("a", 2, 3), ("b", 2, 3), ("b2", 2, 3)]
+        )
+        bank_of = {key: banks[n % 8] for n, key in enumerate(groups)}
 
         ident = sbuf("ident", [P, P], F32)
-        gain_col = sbuf("gain_col", [P, CHUNKS * PACK], BF16)
+        gain_col = sbuf("gain_col", [P, N // P], BF16)
         gain_all = sbuf("gain_all", [P, N], BF16)
         resp_col = sbuf("resp_col", [P, TILES], BF16)
         d_rows = [sbuf("d_rows%d" % i, [P, K], BF16) for i in range(TILES)]
+        d_sorted = [sbuf("d_sorted%d" % i, [P, K // 2], F32) for i in range(TILES)]
         d_pos = sbuf("d_pos", [P, UNITS * K_PASS], BF16)
         d_neg = sbuf("d_neg", [P, UNITS * K_PASS], BF16)
         pos_codes = sbuf("pos_codes", [P, UNITS * P], U32)
@@ -55,11 +62,10 @@ def tile_twelve_lead_ecg_synthesis_s10_kernel(
         neg_codes = sbuf("neg_codes", [P, UNITS * P], U32)
         neg_scales = sbuf("neg_scales", [P, UNITS * P], U8)
         ref_codes = [sbuf("ref_codes%d" % c, [P, PASSES, 2 * BANK], U8) for c in range(CHUNKS)]
-        site_first = [sbuf("site_first%d" % g, [P, BANK], U32) for g in range(PASSES)]
-        site_later = [sbuf("site_later%d" % c, [P, PASSES, BANK], U32) for c in range(1, CHUNKS)]
+        site_codes = [sbuf("site_codes%d" % c, [P, PASSES, BANK], U32) for c in range(CHUNKS)]
         widths = (BANK, N - BANK)
         ref_planes = [sbuf("ref_plane%d" % s, [P, PASSES, w], U8) for s, w in enumerate(widths)]
-        site_planes = [sbuf("site_plane%d" % s, [P, PASSES, w], U8) for s, w in enumerate(widths)]
+        site_plane = sbuf("site_plane", [P, PASSES, N], U8)
         cg = [(c, g) for c in range(CHUNKS) for g in range(PASSES)]
         w_rows = {k: sbuf("w_rows%d_%d" % k, [P, PACK, BANK], BF16) for k in cg}
         w_quads = {k: sbuf("w_quads%d_%d" % k, [P, PACK * BANK], BF16) for k in cg}
@@ -72,16 +78,15 @@ def tile_twelve_lead_ecg_synthesis_s10_kernel(
         ref_hbm = ref_words.bitcast(I32)
         site_hbm = site_words.rearrange("g p n t -> g p (n t)").bitcast(I32)
 
-        def zero_plane(engine, plane):
-            engine.memset(plane[:].rearrange("p g n -> p (g n)").bitcast(I32), 0)
+        def zero_plane(plane):
+            nc.vector.memset(plane[:].rearrange("p g n -> p (g n)").bitcast(I32), 0)
 
-        def load_plane(queue, plane, scales, row, s):
+        def load_plane(plane, scales, row, n0, n1):
             words = scales.bitcast(I32)
-            n0 = 0 if s == 0 else BANK // 4
-            for q in range(4):
-                queue.dma_start(
-                    out=plane[32 * q + row : 32 * q + row + 4, :, :].bitcast(I32),
-                    in_=words[:, 4 * q : 4 * q + 4, n0 : n0 + widths[s] // 4].rearrange("g r n -> r g n"),
+            for r in range(4):
+                nc.sync.dma_start(
+                    out=plane[row + r : P : 32, :, :].bitcast(I32),
+                    in_=words[:, r:16:4, n0 // 4 : n1 // 4].rearrange("g q n -> q g n"),
                 )
 
         def load_ref(c):
@@ -91,79 +96,76 @@ def tile_twelve_lead_ecg_synthesis_s10_kernel(
             )
 
         def load_site(c):
-            cols = slice(c * BANK, (c + 1) * BANK)
-            if c == 0:
-                for g in range(PASSES):
-                    nc.sync.dma_start(out=site_first[g][:].bitcast(I32), in_=site_hbm[g, :, cols])
-            else:
-                nc.sync.dma_start(
-                    out=site_later[c - 1][:].bitcast(I32), in_=site_hbm[:, :, cols].rearrange("g p n -> p g n")
-                )
+            nc.sync.dma_start(
+                out=site_codes[c][:].bitcast(I32),
+                in_=site_hbm[:, :, c * BANK : (c + 1) * BANK].rearrange("g p n -> p g n"),
+            )
 
-        def load_breath(c):
-            for g in range(PASSES):
-                rows = w_breath[g * K_PASS : (g + 1) * K_PASS, c * BANK : (c + 1) * BANK]
-                nc.sync.dma_start(out=w_rows[c, g][:], in_=rows.rearrange("(p j) n -> p j n", j=PACK))
+        def load_breath(c, g):
+            rows = w_breath[g * K_PASS : (g + 1) * K_PASS, c * BANK : (c + 1) * BANK]
+            nc.sync.dma_start(out=w_rows[c, g][:], in_=rows.rearrange("(p j) n -> p j n", j=PACK))
 
-        nc.scalar.dma_start(
-            out=gain_col[:].rearrange("p (c j) -> p c j", j=PACK),
-            in_=gain.rearrange("(c p j) -> p c j", p=P, j=PACK),
-        )
-        nc.scalar.dma_start(out=resp_col[:], in_=resp.rearrange("(p i) -> p i", i=TILES))
-        zero_plane(nc.vector, ref_planes[0])
+        nc.scalar.dma_start(out=gain_col[:], in_=gain.rearrange("(p j) -> p j", p=P))
         make_identity(nc, ident[:])
-        zero_plane(nc.gpsimd, site_planes[0])
-        zero_plane(nc.vector, ref_planes[1])
-        zero_plane(nc.vector, site_planes[1])
-        load_plane(nc.gpsimd, site_planes[0], site_scales, SITE_ROW, 0)
+        zero_plane(ref_planes[0])
+        zero_plane(site_plane)
+        zero_plane(ref_planes[1])
         for i in range(TILES):
             nc.sync.dma_start(out=d_rows[i][:], in_=d_hbm[i])
-        load_plane(nc.sync, ref_planes[0], ref_scales, 0, 0)
+        load_plane(ref_planes[0], ref_scales, 0, 0, BANK)
         load_ref(0)
         load_site(0)
-        load_breath(0)
-        load_plane(nc.sync, ref_planes[1], ref_scales, 0, 1)
+        load_plane(site_plane, site_scales, SITE_ROW, 0, N)
+        nc.sync.dma_start(out=resp_col[:], in_=resp.rearrange("(p i) -> p i", i=TILES))
+        for g in range(PASSES):
+            load_breath(0, g)
+        load_plane(ref_planes[1], ref_scales, 0, BANK, N)
         load_ref(1)
         load_site(1)
-        load_plane(nc.sync, site_planes[1], site_scales, SITE_ROW, 1)
-        load_breath(1)
-        load_breath(2)
+        for g in range(PASSES):
+            load_breath(1, g)
         load_ref(2)
+        load_breath(2, 0)
+        load_breath(2, 1)
         load_site(2)
+        load_breath(2, 2)
 
         gain_words = gain_col[:].bitcast(F32)
-        for w in range(2 * CHUNKS):
+        for w in range(GAIN_WORDS):
             nc.tensor.transpose(
-                a_banks[w // 4][:, (w % 4) * P : (w % 4 + 1) * P],
+                banks[6 + w // 4][:, (w % 4) * P : (w % 4 + 1) * P],
                 gain_words[:, w : w + 1].to_broadcast([P, P]),
                 ident[:],
             )
-        for b, count in enumerate((2, 1)):
-            nc.vector.tensor_copy(
-                out=gain_all[:, 2 * b * BANK : (2 * b + count) * BANK]
-                .bitcast(F32)
-                .rearrange("p (c r h) -> p c r h", c=count, h=2),
-                in_=a_banks[b][:, : count * 2 * P].rearrange("p (c h r) -> p c r h", c=count, h=2),
+
+        def spread_gain(b):
+            w0, w1 = 4 * b, min(4 * b + 4, GAIN_WORDS)
+            nc.scalar.copy(
+                out=gain_all[:].bitcast(F32).rearrange("p (r w) -> p r w", w=GAIN_WORDS)[:, :, w0:w1],
+                in_=banks[6 + b][:, : (w1 - w0) * P].rearrange("p (w r) -> p r w", r=P),
             )
 
-        t_banks = b_banks + a_banks[2:]
+        def sort_words(i):
+            nc.vector.tensor_copy(
+                out=d_sorted[i][:].rearrange("p (g h w) -> p g h w", g=PASSES, h=2),
+                in_=d_rows[i][:].bitcast(F32).rearrange("p (g w h) -> p g h w", g=PASSES, h=2),
+            )
 
         def turn(j):
             for u in (2 * j, 2 * j + 1):
                 i, g = divmod(u, PASSES)
-                words = d_rows[i][:].bitcast(F32)
                 for h in range(2):
                     slot = 2 * (u % 2) + h
                     nc.tensor.transpose(
-                        t_banks[j][:, slot * P : (slot + 1) * P],
-                        words[:, 2 * P * g + h : 2 * P * (g + 1) : 2],
+                        banks[j][:, slot * P : (slot + 1) * P],
+                        d_sorted[i][:, (2 * g + h) * P : (2 * g + h + 1) * P],
                         ident[:],
                     )
             nc.scalar.copy(
                 out=d_pos[:, 2 * j * K_PASS : 2 * (j + 1) * K_PASS]
                 .bitcast(F32)
                 .rearrange("p (u r h) -> p u r h", u=2, h=2),
-                in_=t_banks[j][:].rearrange("p (u h r) -> p u r h", u=2, h=2),
+                in_=banks[j][:].rearrange("p (u h r) -> p u r h", u=2, h=2),
             )
 
         def quantize(values, codes, scales, u0, u1):
@@ -190,10 +192,10 @@ def tile_twelve_lead_ecg_synthesis_s10_kernel(
             )
 
         def interleave_scalar(c, g):
-            interleave(nc.scalar.copy, c, g, 0, SCALAR_COLS)
+            interleave(nc.scalar.copy, c, g, 0, SCALAR_COLS[c])
 
         def interleave_vector(c, g):
-            interleave(nc.vector.tensor_copy, c, g, SCALAR_COLS, BANK)
+            interleave(nc.vector.tensor_copy, c, g, SCALAR_COLS[c], BANK)
 
         def quantize_breath(c, g):
             nc.vector.quantize_mx(out=w_codes[c, g][:].bitcast(FP8X4), scales=w_scales[c, g][:], in_=w_quads[c, g][:])
@@ -202,14 +204,16 @@ def tile_twelve_lead_ecg_synthesis_s10_kernel(
             s = min(c, 1)
             return s, slice((c - s) * BANK, (c - s + 1) * BANK)
 
+        def unit(i, g):
+            return slice((PASSES * i + g) * P, (PASSES * i + g + 1) * P)
+
         def mm_ref(c, i):
             s, cols = plane_cols(c)
             for g in range(PASSES):
-                u = slice((PASSES * i + g) * P, (PASSES * i + g + 1) * P)
                 nc.tensor.matmul_mx(
-                    out=a_banks[i][:],
-                    lhsT=pos_codes[:, u].bitcast(FP8X4),
-                    lhsT_scale=pos_scales[:, u],
+                    out=bank_of["a", c, i][:],
+                    lhsT=pos_codes[:, unit(i, g)].bitcast(FP8X4),
+                    lhsT_scale=pos_scales[:, unit(i, g)],
                     rhs=ref_codes[c][:, g, :].bitcast(FP4X4),
                     rhs_scale=ref_planes[s][:, g, cols],
                     start=(g == 0),
@@ -217,134 +221,156 @@ def tile_twelve_lead_ecg_synthesis_s10_kernel(
                 )
 
         def mm_site(c, i):
-            s, cols = plane_cols(c)
             for g in range(PASSES):
-                u = slice((PASSES * i + g) * P, (PASSES * i + g + 1) * P)
-                codes = site_first[g][:] if c == 0 else site_later[c - 1][:, g, :]
                 nc.tensor.matmul_mx(
-                    out=a_banks[i][:],
-                    lhsT=neg_codes[:, u].bitcast(FP8X4),
-                    lhsT_scale=neg_scales[:, u],
-                    rhs=codes.bitcast(FP8X4),
-                    rhs_scale=site_planes[s][SITE_ROW:, g, cols],
+                    out=bank_of["a", c, i][:],
+                    lhsT=neg_codes[:, unit(i, g)].bitcast(FP8X4),
+                    lhsT_scale=neg_scales[:, unit(i, g)],
+                    rhs=site_codes[c][:, g, :].bitcast(FP8X4),
+                    rhs_scale=site_plane[SITE_ROW:, g, c * BANK : (c + 1) * BANK],
                     start=False,
-                    stop=(g == PASSES - 1),
-                )
-
-        def mm_breath(c, i, bank, cols):
-            for g in range(PASSES):
-                u = slice((PASSES * i + g) * P, (PASSES * i + g + 1) * P)
-                nc.tensor.matmul_mx(
-                    out=bank[:, cols],
-                    lhsT=pos_codes[:, u].bitcast(FP8X4),
-                    lhsT_scale=pos_scales[:, u],
-                    rhs=w_codes[c, g][:, cols].bitcast(FP8X4),
-                    rhs_scale=w_scales[c, g][:, cols],
-                    start=(g == 0),
                     stop=(g == PASSES - 1),
                 )
 
         whole = slice(0, BANK)
 
-        def park(c, i):
-            nc.scalar.copy(out=result[c, i][:], in_=a_banks[i][:])
+        def mm_breath_pass(c, i, g, kind="b", cols=whole):
+            nc.tensor.matmul_mx(
+                out=bank_of[kind, c, i][:, cols],
+                lhsT=pos_codes[:, unit(i, g)].bitcast(FP8X4),
+                lhsT_scale=pos_scales[:, unit(i, g)],
+                rhs=w_codes[c, g][:, cols].bitcast(FP8X4),
+                rhs_scale=w_scales[c, g][:, cols],
+                start=(g == 0),
+                stop=(g == PASSES - 1),
+            )
 
-        def combine(c, i, bank, cols):
+        def mm_breath(c, i, kind="b", cols=whole):
+            for g in range(PASSES):
+                mm_breath_pass(c, i, g, kind, cols)
+
+        def mm_terminal(c, tiles):
+            for i in tiles:
+                mm_ref(c, i)
+            for i in tiles:
+                mm_site(c, i)
+
+        def park(c, i):
+            nc.scalar.copy(out=result[c, i][:], in_=bank_of["a", c, i][:])
+
+        def combine(c, i, kind="b", cols=whole):
             nc.vector.scalar_tensor_tensor(
                 out=result[c, i][:, cols],
-                in0=bank[:, cols],
+                in0=bank_of[kind, c, i][:, cols],
                 scalar=resp_col[:, i : i + 1],
                 in1=result[c, i][:, cols],
                 op0=ALU.mult,
                 op1=ALU.subtract,
             )
 
-        def finish(c, i, cols):
+        def finish(c, i, cols=whole):
             n = slice(c * BANK + cols.start, c * BANK + cols.stop)
             nc.vector.tensor_tensor(
                 out=result[c, i][:, cols], in0=result[c, i][:, cols], in1=gain_all[:, n], op=ALU.mult
             )
             nc.sync.dma_start(out=out_hbm[i][:, n], in_=result[c, i][:, cols])
 
-        for j in range(UNITS // 2):
-            turn(j)
-            quantize_pos(j)
-            if j % 2 == 1:
-                negate(j // 2)
-            elif j > 0:
-                quantize_neg(j // 2 - 1)
-
-        for g in range(PASSES):
-            interleave_scalar(0, g)
-        interleave_vector(0, 0)
+        sort_words(0)
+        turn(0)
+        sort_words(1)
+        turn(1)
+        turn(2)
+        quantize_pos(0)
+        sort_words(2)
+        turn(3)
+        quantize_pos(1)
+        quantize_pos(2)
+        sort_words(3)
+        turn(4)
+        turn(5)
+        quantize_pos(3)
+        negate(0)
+        quantize_pos(4)
+        quantize_pos(5)
+        quantize_neg(0)
+        negate(1)
+        negate(2)
+        quantize_neg(1)
         quantize_neg(2)
+        spread_gain(0)
+        spread_gain(1)
+
+        mm_terminal(0, range(TILES))
+        interleave_scalar(0, 0)
+        park(0, 0)
+        interleave_scalar(0, 1)
+        interleave_scalar(0, 2)
+        for i in range(1, TILES):
+            park(0, i)
+        interleave_vector(0, 0)
         interleave_vector(0, 1)
         quantize_breath(0, 0)
         interleave_vector(0, 2)
         quantize_breath(0, 1)
         quantize_breath(0, 2)
-        for i in range(TILES):
-            mm_ref(0, i)
-        for i in range(TILES):
-            mm_site(0, i)
-            park(0, i)
-        for i in range(TILES):
-            mm_breath(0, i, b_banks[i], whole)
-            combine(0, i, b_banks[i], whole)
-            if i > 0:
-                finish(0, i - 1, whole)
+        for g in range(PASSES):
+            for i in range(TILES):
+                mm_breath_pass(0, i, g)
 
+        mm_terminal(1, range(TILES))
         for g in range(PASSES):
             interleave_scalar(1, g)
+        combine(0, 0)
+        for i in range(1, TILES):
+            combine(0, i)
+            finish(0, i - 1)
         interleave_vector(1, 0)
-        finish(0, TILES - 1, whole)
+        finish(0, TILES - 1)
         interleave_vector(1, 1)
         quantize_breath(1, 0)
         interleave_vector(1, 2)
         quantize_breath(1, 1)
-        interleave_vector(2, 0)
         quantize_breath(1, 2)
-        interleave_vector(2, 1)
-        interleave_vector(2, 2)
-        for i in range(TILES):
-            mm_ref(1, i)
-            mm_site(1, i)
-            park(1, i)
-            if i == 1:
-                interleave_scalar(2, 0)
+        park(1, 0)
+        park(1, 1)
+        interleave_scalar(2, 0)
+        park(1, 2)
+        park(1, 3)
         interleave_scalar(2, 1)
         interleave_scalar(2, 2)
-        quantize_breath(2, 0)
         for i in range(TILES):
-            mm_breath(1, i, b_banks[i], whole)
-            combine(1, i, b_banks[i], whole)
-            if i > 0:
-                finish(1, i - 1, whole)
-        quantize_breath(2, 1)
-        finish(1, TILES - 1, whole)
-        quantize_breath(2, 2)
+            mm_breath(1, i)
 
-        for i in range(2):
-            mm_ref(2, i)
-            mm_site(2, i)
+        mm_terminal(2, range(3))
+        combine(1, 0)
+        interleave_vector(2, 0)
+        finish(1, 0)
+        combine(1, 1)
+        interleave_vector(2, 1)
+        finish(1, 1)
+        combine(1, 2)
+        quantize_breath(2, 0)
+        combine(1, 3)
+        quantize_breath(2, 1)
+        interleave_vector(2, 2)
+        finish(1, 2)
+        quantize_breath(2, 2)
+        finish(1, 3)
+        for i in range(3):
             park(2, i)
-        for i in range(2):
-            mm_breath(2, i, b_banks[i], whole)
-            combine(2, i, b_banks[i], whole)
-        for i in range(2):
-            finish(2, i, whole)
-        mm_ref(2, 2)
-        mm_site(2, 2)
-        park(2, 2)
-        mm_breath(2, 2, b_banks[2], whole)
-        combine(2, 2, b_banks[2], whole)
-        finish(2, 2, whole)
-        mm_ref(2, 3)
-        mm_site(2, 3)
+        for i in range(3):
+            mm_breath(2, i)
+        mm_terminal(2, [3])
         park(2, 3)
-        halves = ((b_banks[3], slice(0, BANK // 2)), (a_banks[0], slice(BANK // 2, BANK)))
-        for bank, cols in halves:
-            mm_breath(2, 3, bank, cols)
-            combine(2, 3, bank, cols)
-        for bank, cols in halves:
+        combine(2, 0)
+        combine(2, 1)
+        finish(2, 0)
+        combine(2, 2)
+        finish(2, 1)
+        finish(2, 2)
+        halves = (("b", slice(0, BANK // 2)), ("b2", slice(BANK // 2, BANK)))
+        for kind, cols in halves:
+            mm_breath(2, 3, kind, cols)
+            combine(2, 3, kind, cols)
+        for kind, cols in halves:
             finish(2, 3, cols)

@@ -14,6 +14,7 @@ U8 = mybir.dt.uint8
 FP8X4 = mybir.dt.float8_e4m3fn_x4
 FP4X4 = mybir.dt.float4_e2m1fn_x4
 ALU = mybir.AluOpType
+ACT = mybir.ActivationFunctionType
 
 P = 128
 PACK = 4
@@ -24,7 +25,7 @@ BANK = 512
 CHUNKS = N // BANK
 UNITS = TILES * PASSES
 SITE_ROW = 4
-SCALAR_COLS = (192, 320, 384)
+SCALAR_COLS = (224, 384, 384)
 GAIN_WORDS = N // P // 2
 
 
@@ -41,18 +42,14 @@ def tile_twelve_lead_ecg_synthesis_s10_kernel(
             return sb.tile(shape, dtype, name=name, align_bytes=64)
 
         banks = [ps.tile([P, BANK], F32, name="bank%d" % b) for b in range(8)]
-        groups = (
-            [("a", 0, i) for i in range(TILES)] + [("b", 0, i) for i in range(TILES)]
-            + [("a", 1, i) for i in range(TILES)] + [("b", 1, i) for i in range(TILES)]
-            + [("a", 2, i) for i in range(3)] + [("b", 2, i) for i in range(3)]
-            + [("a", 2, 3), ("b", 2, 3), ("b2", 2, 3)]
-        )
-        bank_of = {key: banks[n % 8] for n, key in enumerate(groups)}
+        bank_of = {(kind, c, i): banks[i + (TILES if kind == "b" else 0)] for kind in "ab" for c in range(CHUNKS) for i in range(TILES)}
+        bank_of["b2", 2, 3] = banks[0]
 
         ident = sbuf("ident", [P, P], F32)
         gain_col = sbuf("gain_col", [P, N // P], BF16)
         gain_all = sbuf("gain_all", [P, N], BF16)
         resp_col = sbuf("resp_col", [P, TILES], BF16)
+        resp_f32 = sbuf("resp_f32", [P, TILES], F32)
         d_rows = [sbuf("d_rows%d" % i, [P, K], BF16) for i in range(TILES)]
         d_sorted = [sbuf("d_sorted%d" % i, [P, K // 2], F32) for i in range(TILES)]
         d_pos = sbuf("d_pos", [P, UNITS * K_PASS], BF16)
@@ -65,7 +62,7 @@ def tile_twelve_lead_ecg_synthesis_s10_kernel(
         site_codes = [sbuf("site_codes%d" % c, [P, PASSES, BANK], U32) for c in range(CHUNKS)]
         widths = (BANK, N - BANK)
         ref_planes = [sbuf("ref_plane%d" % s, [P, PASSES, w], U8) for s, w in enumerate(widths)]
-        site_plane = sbuf("site_plane", [P, PASSES, N], U8)
+        site_planes = [sbuf("site_plane%d" % s, [P, PASSES, w], U8) for s, w in enumerate(widths)]
         cg = [(c, g) for c in range(CHUNKS) for g in range(PASSES)]
         w_rows = {k: sbuf("w_rows%d_%d" % k, [P, PACK, BANK], BF16) for k in cg}
         w_quads = {k: sbuf("w_quads%d_%d" % k, [P, PACK * BANK], BF16) for k in cg}
@@ -107,28 +104,30 @@ def tile_twelve_lead_ecg_synthesis_s10_kernel(
 
         nc.scalar.dma_start(out=gain_col[:], in_=gain.rearrange("(p j) -> p j", p=P))
         make_identity(nc, ident[:])
-        zero_plane(ref_planes[0])
-        zero_plane(site_plane)
-        zero_plane(ref_planes[1])
+        for s in range(2):
+            zero_plane(ref_planes[s])
+            zero_plane(site_planes[s])
         for i in range(TILES):
             nc.sync.dma_start(out=d_rows[i][:], in_=d_hbm[i])
         load_plane(ref_planes[0], ref_scales, 0, 0, BANK)
         load_ref(0)
         load_site(0)
-        load_plane(site_plane, site_scales, SITE_ROW, 0, N)
+        load_plane(site_planes[0], site_scales, SITE_ROW, 0, BANK)
         nc.sync.dma_start(out=resp_col[:], in_=resp.rearrange("(p i) -> p i", i=TILES))
         for g in range(PASSES):
             load_breath(0, g)
         load_plane(ref_planes[1], ref_scales, 0, BANK, N)
         load_ref(1)
+        load_breath(1, 0)
+        load_breath(1, 1)
         load_site(1)
-        for g in range(PASSES):
-            load_breath(1, g)
-        load_ref(2)
+        load_plane(site_planes[1], site_scales, SITE_ROW, BANK, N)
+        load_breath(1, 2)
         load_breath(2, 0)
         load_breath(2, 1)
-        load_site(2)
+        load_ref(2)
         load_breath(2, 2)
+        load_site(2)
 
         gain_words = gain_col[:].bitcast(F32)
         for w in range(GAIN_WORDS):
@@ -221,13 +220,14 @@ def tile_twelve_lead_ecg_synthesis_s10_kernel(
                 )
 
         def mm_site(c, i):
+            s, cols = plane_cols(c)
             for g in range(PASSES):
                 nc.tensor.matmul_mx(
                     out=bank_of["a", c, i][:],
                     lhsT=neg_codes[:, unit(i, g)].bitcast(FP8X4),
                     lhsT_scale=neg_scales[:, unit(i, g)],
                     rhs=site_codes[c][:, g, :].bitcast(FP8X4),
-                    rhs_scale=site_plane[SITE_ROW:, g, c * BANK : (c + 1) * BANK],
+                    rhs_scale=site_planes[s][SITE_ROW:, g, cols],
                     start=False,
                     stop=(g == PASSES - 1),
                 )
@@ -255,8 +255,8 @@ def tile_twelve_lead_ecg_synthesis_s10_kernel(
             for i in tiles:
                 mm_site(c, i)
 
-        def park(c, i):
-            nc.scalar.copy(out=result[c, i][:], in_=bank_of["a", c, i][:])
+        def park(c, i, cols=whole, copy=nc.scalar.copy):
+            copy(out=result[c, i][:, cols], in_=bank_of["a", c, i][:, cols])
 
         def combine(c, i, kind="b", cols=whole):
             nc.vector.scalar_tensor_tensor(
@@ -268,30 +268,41 @@ def tile_twelve_lead_ecg_synthesis_s10_kernel(
                 op1=ALU.subtract,
             )
 
-        def finish(c, i, cols=whole):
-            n = slice(c * BANK + cols.start, c * BANK + cols.stop)
+        def park_breath(c, i):
+            nc.scalar.activation(
+                out=result[c, i][:], in_=bank_of["b", c, i][:], func=ACT.Copy, scale=resp_f32[:, i : i + 1]
+            )
+
+        def subtract(c, i, cols=whole):
             nc.vector.tensor_tensor(
+                out=result[c, i][:, cols], in0=result[c, i][:, cols], in1=bank_of["a", c, i][:, cols], op=ALU.subtract
+            )
+
+        def mm_breath_by_pass(c):
+            for g in range(PASSES):
+                for i in range(TILES):
+                    mm_breath_pass(c, i, g)
+
+        def finish(c, i, cols=whole, engine=nc.vector):
+            n = slice(c * BANK + cols.start, c * BANK + cols.stop)
+            engine.tensor_tensor(
                 out=result[c, i][:, cols], in0=result[c, i][:, cols], in1=gain_all[:, n], op=ALU.mult
             )
             nc.sync.dma_start(out=out_hbm[i][:, n], in_=result[c, i][:, cols])
 
         sort_words(0)
-        turn(0)
         sort_words(1)
-        turn(1)
-        turn(2)
-        quantize_pos(0)
         sort_words(2)
-        turn(3)
-        quantize_pos(1)
-        quantize_pos(2)
+        for j in range(4):
+            turn(j)
+        quantize_pos(0)
         sort_words(3)
         turn(4)
         turn(5)
-        quantize_pos(3)
+        quantize_pos(1)
         negate(0)
-        quantize_pos(4)
-        quantize_pos(5)
+        for j in range(2, 6):
+            quantize_pos(j)
         quantize_neg(0)
         negate(1)
         negate(2)
@@ -302,8 +313,8 @@ def tile_twelve_lead_ecg_synthesis_s10_kernel(
 
         mm_terminal(0, range(TILES))
         interleave_scalar(0, 0)
-        park(0, 0)
         interleave_scalar(0, 1)
+        park(0, 0)
         interleave_scalar(0, 2)
         for i in range(1, TILES):
             park(0, i)
@@ -313,46 +324,47 @@ def tile_twelve_lead_ecg_synthesis_s10_kernel(
         interleave_vector(0, 2)
         quantize_breath(0, 1)
         quantize_breath(0, 2)
-        for g in range(PASSES):
-            for i in range(TILES):
-                mm_breath_pass(0, i, g)
+        mm_breath_by_pass(0)
 
         mm_terminal(1, range(TILES))
         for g in range(PASSES):
             interleave_scalar(1, g)
-        combine(0, 0)
-        for i in range(1, TILES):
-            combine(0, i)
-            finish(0, i - 1)
         interleave_vector(1, 0)
-        finish(0, TILES - 1)
+        combine(0, 0)
         interleave_vector(1, 1)
+        combine(0, 1)
         quantize_breath(1, 0)
-        interleave_vector(1, 2)
+        finish(0, 0)
+        combine(0, 2)
+        finish(0, 1)
+        combine(0, 3)
         quantize_breath(1, 1)
+        finish(0, 2)
+        interleave_vector(1, 2)
+        finish(0, 3)
         quantize_breath(1, 2)
         park(1, 0)
-        park(1, 1)
         interleave_scalar(2, 0)
+        park(1, 1)
         park(1, 2)
-        park(1, 3)
         interleave_scalar(2, 1)
+        park(1, 3)
         interleave_scalar(2, 2)
         for i in range(TILES):
             mm_breath(1, i)
 
         mm_terminal(2, range(3))
-        combine(1, 0)
         interleave_vector(2, 0)
-        finish(1, 0)
-        combine(1, 1)
         interleave_vector(2, 1)
-        finish(1, 1)
-        combine(1, 2)
+        combine(1, 0)
         quantize_breath(2, 0)
+        combine(1, 1)
+        finish(1, 0)
+        combine(1, 2)
+        interleave_vector(2, 2)
         combine(1, 3)
         quantize_breath(2, 1)
-        interleave_vector(2, 2)
+        finish(1, 1)
         finish(1, 2)
         quantize_breath(2, 2)
         finish(1, 3)
@@ -361,14 +373,15 @@ def tile_twelve_lead_ecg_synthesis_s10_kernel(
         for i in range(3):
             mm_breath(2, i)
         mm_terminal(2, [3])
-        park(2, 3)
+        halves = (("b", slice(0, BANK // 2)), ("b2", slice(BANK // 2, BANK)))
+        for kind, cols in halves:
+            park(2, 3, cols)
         combine(2, 0)
         combine(2, 1)
         finish(2, 0)
         combine(2, 2)
         finish(2, 1)
         finish(2, 2)
-        halves = (("b", slice(0, BANK // 2)), ("b2", slice(BANK // 2, BANK)))
         for kind, cols in halves:
             mm_breath(2, 3, kind, cols)
             combine(2, 3, kind, cols)

@@ -14,7 +14,6 @@ U8 = mybir.dt.uint8
 FP8X4 = mybir.dt.float8_e4m3fn_x4
 FP4X4 = mybir.dt.float4_e2m1fn_x4
 ALU = mybir.AluOpType
-ACT = mybir.ActivationFunctionType
 
 P = 128
 PACK = 4
@@ -25,7 +24,7 @@ BANK = 512
 CHUNKS = N // BANK
 UNITS = TILES * PASSES
 SITE_ROW = 4
-SCALAR_COLS = (224, 384, 384)
+SCALAR_COLS = (224, 320, 320)
 GAIN_WORDS = N // P // 2
 
 
@@ -39,7 +38,7 @@ def tile_twelve_lead_ecg_synthesis_s10_kernel(
         ctx.enter_context(tc.manual_schedule())
 
         def sbuf(name, shape, dtype):
-            return sb.tile(shape, dtype, name=name, align_bytes=64)
+            return sb.tile(shape, dtype, name=name, align_bytes=256)
 
         banks = [ps.tile([P, BANK], F32, name="bank%d" % b) for b in range(8)]
         bank_of = {(kind, c, i): banks[i + (TILES if kind == "b" else 0)] for kind in "ab" for c in range(CHUNKS) for i in range(TILES)}
@@ -49,7 +48,6 @@ def tile_twelve_lead_ecg_synthesis_s10_kernel(
         gain_col = sbuf("gain_col", [P, N // P], BF16)
         gain_all = sbuf("gain_all", [P, N], BF16)
         resp_col = sbuf("resp_col", [P, TILES], BF16)
-        resp_f32 = sbuf("resp_f32", [P, TILES], F32)
         d_rows = [sbuf("d_rows%d" % i, [P, K], BF16) for i in range(TILES)]
         d_sorted = [sbuf("d_sorted%d" % i, [P, K // 2], F32) for i in range(TILES)]
         d_pos = sbuf("d_pos", [P, UNITS * K_PASS], BF16)
@@ -107,10 +105,11 @@ def tile_twelve_lead_ecg_synthesis_s10_kernel(
         for s in range(2):
             zero_plane(ref_planes[s])
             zero_plane(site_planes[s])
-        for i in range(TILES):
+        for i in range(TILES - 1):
             nc.sync.dma_start(out=d_rows[i][:], in_=d_hbm[i])
         load_plane(ref_planes[0], ref_scales, 0, 0, BANK)
         load_ref(0)
+        nc.sync.dma_start(out=d_rows[TILES - 1][:], in_=d_hbm[TILES - 1])
         load_site(0)
         load_plane(site_planes[0], site_scales, SITE_ROW, 0, BANK)
         nc.sync.dma_start(out=resp_col[:], in_=resp.rearrange("(p i) -> p i", i=TILES))
@@ -120,8 +119,8 @@ def tile_twelve_lead_ecg_synthesis_s10_kernel(
         load_ref(1)
         load_breath(1, 0)
         load_breath(1, 1)
-        load_site(1)
         load_plane(site_planes[1], site_scales, SITE_ROW, BANK, N)
+        load_site(1)
         load_breath(1, 2)
         load_breath(2, 0)
         load_breath(2, 1)
@@ -268,16 +267,6 @@ def tile_twelve_lead_ecg_synthesis_s10_kernel(
                 op1=ALU.subtract,
             )
 
-        def park_breath(c, i):
-            nc.scalar.activation(
-                out=result[c, i][:], in_=bank_of["b", c, i][:], func=ACT.Copy, scale=resp_f32[:, i : i + 1]
-            )
-
-        def subtract(c, i, cols=whole):
-            nc.vector.tensor_tensor(
-                out=result[c, i][:, cols], in0=result[c, i][:, cols], in1=bank_of["a", c, i][:, cols], op=ALU.subtract
-            )
-
         def mm_breath_by_pass(c):
             for g in range(PASSES):
                 for i in range(TILES):
@@ -295,23 +284,29 @@ def tile_twelve_lead_ecg_synthesis_s10_kernel(
         sort_words(2)
         for j in range(4):
             turn(j)
+        spread_gain(0)
+        spread_gain(1)
         quantize_pos(0)
+        quantize_pos(1)
+        mm_ref(0, 0)
+        negate(0)
+        quantize_pos(2)
         sort_words(3)
         turn(4)
         turn(5)
-        quantize_pos(1)
-        negate(0)
-        for j in range(2, 6):
-            quantize_pos(j)
+        quantize_pos(3)
         quantize_neg(0)
         negate(1)
-        negate(2)
+        quantize_pos(4)
         quantize_neg(1)
+        quantize_pos(5)
+        negate(2)
         quantize_neg(2)
-        spread_gain(0)
-        spread_gain(1)
 
-        mm_terminal(0, range(TILES))
+        for i in range(1, TILES):
+            mm_ref(0, i)
+        for i in range(TILES):
+            mm_site(0, i)
         interleave_scalar(0, 0)
         interleave_scalar(0, 1)
         park(0, 0)

from contextlib import ExitStack

import concourse.mybir as mybir
from concourse.masks import make_identity

T, K, N = 512, 1536, 1536
FLOPS = 3 * 2 * T * K * N

F32 = mybir.dt.float32
BF16 = mybir.dt.bfloat16
I32 = mybir.dt.int32
U32 = mybir.dt.uint32
U8 = mybir.dt.uint8
FP8X4 = mybir.dt.float8_e4m3fn_x4
FP4X4 = mybir.dt.float4_e2m1fn_x4
ALU = mybir.AluOpType

P = 128
PACK = 4
K_PASS = P * PACK
PASSES = K // K_PASS
TILES = T // P
BANK = 512
CHUNKS = N // BANK
UNITS = TILES * PASSES
SITE_ROW = 4
SCALAR_COLS = (224, 320, 320)
GAIN_WORDS = N // P // 2


def tile_twelve_lead_ecg_synthesis_s10_kernel(
    tc, dipoles, ref_words, ref_scales, site_words, site_scales, w_breath, resp, gain, out
):
    nc = tc.nc
    with ExitStack() as ctx:
        sb = ctx.enter_context(tc.tile_pool(name="sb", bufs=1))
        ps = ctx.enter_context(tc.psum_pool(name="ps", bufs=1))
        ctx.enter_context(tc.manual_schedule())

        def sbuf(name, shape, dtype):
            return sb.tile(shape, dtype, name=name, align_bytes=256)

        banks = [ps.tile([P, BANK], F32, name="bank%d" % b) for b in range(8)]
        bank_of = {(kind, c, i): banks[i + (TILES if kind == "b" else 0)] for kind in "ab" for c in range(CHUNKS) for i in range(TILES)}
        bank_of["b2", 2, 3] = banks[0]

        ident = sbuf("ident", [P, P], F32)
        gain_col = sbuf("gain_col", [P, N // P], BF16)
        gain_all = sbuf("gain_all", [P, N], BF16)
        resp_col = sbuf("resp_col", [P, TILES], BF16)
        d_rows = [sbuf("d_rows%d" % i, [P, K], BF16) for i in range(TILES)]
        d_sorted = [sbuf("d_sorted%d" % i, [P, K // 2], F32) for i in range(TILES)]
        d_pos = sbuf("d_pos", [P, UNITS * K_PASS], BF16)
        d_neg = sbuf("d_neg", [P, UNITS * K_PASS], BF16)
        pos_codes = sbuf("pos_codes", [P, UNITS * P], U32)
        pos_scales = sbuf("pos_scales", [P, UNITS * P], U8)
        neg_codes = sbuf("neg_codes", [P, UNITS * P], U32)
        neg_scales = sbuf("neg_scales", [P, UNITS * P], U8)
        ref_codes = [sbuf("ref_codes%d" % c, [P, PASSES, 2 * BANK], U8) for c in range(CHUNKS)]
        site_codes = [sbuf("site_codes%d" % c, [P, PASSES, BANK], U32) for c in range(CHUNKS)]
        widths = (BANK, N - BANK)
        ref_planes = [sbuf("ref_plane%d" % s, [P, PASSES, w], U8) for s, w in enumerate(widths)]
        site_planes = [sbuf("site_plane%d" % s, [P, PASSES, w], U8) for s, w in enumerate(widths)]
        cg = [(c, g) for c in range(CHUNKS) for g in range(PASSES)]
        w_rows = {k: sbuf("w_rows%d_%d" % k, [P, PACK, BANK], BF16) for k in cg}
        w_quads = {k: sbuf("w_quads%d_%d" % k, [P, PACK * BANK], BF16) for k in cg}
        w_codes = {k: sbuf("w_codes%d_%d" % k, [P, BANK], U32) for k in cg}
        w_scales = {k: sbuf("w_scales%d_%d" % k, [P, BANK], U8) for k in cg}
        result = {(c, i): sbuf("result%d_%d" % (c, i), [P, BANK], F32) for c in range(CHUNKS) for i in range(TILES)}

        d_hbm = dipoles.rearrange("(p i) k -> i p k", i=TILES)
        out_hbm = out.rearrange("(p i) n -> i p n", i=TILES)
        ref_hbm = ref_words.bitcast(I32)
        site_hbm = site_words.rearrange("g p n t -> g p (n t)").bitcast(I32)

        def zero_plane(plane):
            nc.vector.memset(plane[:].rearrange("p g n -> p (g n)").bitcast(I32), 0)

        def load_plane(plane, scales, row, n0, n1):
            words = scales.bitcast(I32)
            for r in range(4):
                nc.sync.dma_start(
                    out=plane[row + r : P : 32, :, :].bitcast(I32),
                    in_=words[:, r:16:4, n0 // 4 : n1 // 4].rearrange("g q n -> q g n"),
                )

        def load_ref(c):
            nc.sync.dma_start(
                out=ref_codes[c][:].bitcast(I32),
                in_=ref_hbm[:, :, c * BANK // 2 : (c + 1) * BANK // 2].rearrange("g p w -> p g w"),
            )

        def load_site(c):
            nc.sync.dma_start(
                out=site_codes[c][:].bitcast(I32),
                in_=site_hbm[:, :, c * BANK : (c + 1) * BANK].rearrange("g p n -> p g n"),
            )

        def load_breath(c, g):
            rows = w_breath[g * K_PASS : (g + 1) * K_PASS, c * BANK : (c + 1) * BANK]
            nc.sync.dma_start(out=w_rows[c, g][:], in_=rows.rearrange("(p j) n -> p j n", j=PACK))

        nc.scalar.dma_start(out=gain_col[:], in_=gain.rearrange("(p j) -> p j", p=P))
        make_identity(nc, ident[:])
        for s in range(2):
            zero_plane(ref_planes[s])
            zero_plane(site_planes[s])
        for i in range(TILES - 1):
            nc.sync.dma_start(out=d_rows[i][:], in_=d_hbm[i])
        load_plane(ref_planes[0], ref_scales, 0, 0, BANK)
        load_ref(0)
        nc.sync.dma_start(out=d_rows[TILES - 1][:], in_=d_hbm[TILES - 1])
        load_site(0)
        load_plane(site_planes[0], site_scales, SITE_ROW, 0, BANK)
        nc.sync.dma_start(out=resp_col[:], in_=resp.rearrange("(p i) -> p i", i=TILES))
        for g in range(PASSES):
            load_breath(0, g)
        load_plane(ref_planes[1], ref_scales, 0, BANK, N)
        load_ref(1)
        load_breath(1, 0)
        load_breath(1, 1)
        load_plane(site_planes[1], site_scales, SITE_ROW, BANK, N)
        load_site(1)
        load_breath(1, 2)
        load_breath(2, 0)
        load_breath(2, 1)
        load_ref(2)
        load_breath(2, 2)
        load_site(2)

        gain_words = gain_col[:].bitcast(F32)
        for w in range(GAIN_WORDS):
            nc.tensor.transpose(
                banks[6 + w // 4][:, (w % 4) * P : (w % 4 + 1) * P],
                gain_words[:, w : w + 1].to_broadcast([P, P]),
                ident[:],
            )

        def spread_gain(b):
            w0, w1 = 4 * b, min(4 * b + 4, GAIN_WORDS)
            nc.scalar.copy(
                out=gain_all[:].bitcast(F32).rearrange("p (r w) -> p r w", w=GAIN_WORDS)[:, :, w0:w1],
                in_=banks[6 + b][:, : (w1 - w0) * P].rearrange("p (w r) -> p r w", r=P),
            )

        def sort_words(i):
            nc.vector.tensor_copy(
                out=d_sorted[i][:].rearrange("p (g h w) -> p g h w", g=PASSES, h=2),
                in_=d_rows[i][:].bitcast(F32).rearrange("p (g w h) -> p g h w", g=PASSES, h=2),
            )

        def turn(j):
            for u in (2 * j, 2 * j + 1):
                i, g = divmod(u, PASSES)
                for h in range(2):
                    slot = 2 * (u % 2) + h
                    nc.tensor.transpose(
                        banks[j][:, slot * P : (slot + 1) * P],
                        d_sorted[i][:, (2 * g + h) * P : (2 * g + h + 1) * P],
                        ident[:],
                    )
            nc.scalar.copy(
                out=d_pos[:, 2 * j * K_PASS : 2 * (j + 1) * K_PASS]
                .bitcast(F32)
                .rearrange("p (u r h) -> p u r h", u=2, h=2),
                in_=banks[j][:].rearrange("p (u h r) -> p u r h", u=2, h=2),
            )

        def quantize(values, codes, scales, u0, u1):
            nc.vector.quantize_mx(
                out=codes[:, u0 * P : u1 * P].bitcast(FP8X4),
                scales=scales[:, u0 * P : u1 * P],
                in_=values[:, u0 * K_PASS : u1 * K_PASS],
            )

        def quantize_pos(j):
            quantize(d_pos, pos_codes, pos_scales, 2 * j, 2 * j + 2)

        def negate(m):
            cols = slice(4 * m * K_PASS, 4 * (m + 1) * K_PASS)
            nc.vector.tensor_scalar_mul(out=d_neg[:, cols], in0=d_pos[:, cols], scalar1=-1.0)

        def quantize_neg(m):
            quantize(d_neg, neg_codes, neg_scales, 4 * m, 4 * m + 4)

        def interleave(copy, c, g, n0, n1):
            copy(
                out=w_quads[c, g][:, PACK * n0 : PACK * n1].rearrange("p (m i t) -> p m t i", i=4, t=PACK),
                in_=w_rows[c, g][:, :, n0:n1].rearrange("p t (m i) -> p m t i", i=4),
            )

        def interleave_scalar(c, g):
            interleave(nc.scalar.copy, c, g, 0, SCALAR_COLS[c])

        def interleave_vector(c, g):
            interleave(nc.vector.tensor_copy, c, g, SCALAR_COLS[c], BANK)

        def quantize_breath(c, g):
            nc.vector.quantize_mx(out=w_codes[c, g][:].bitcast(FP8X4), scales=w_scales[c, g][:], in_=w_quads[c, g][:])

        def plane_cols(c):
            s = min(c, 1)
            return s, slice((c - s) * BANK, (c - s + 1) * BANK)

        def unit(i, g):
            return slice((PASSES * i + g) * P, (PASSES * i + g + 1) * P)

        def mm_ref(c, i):
            s, cols = plane_cols(c)
            for g in range(PASSES):
                nc.tensor.matmul_mx(
                    out=bank_of["a", c, i][:],
                    lhsT=pos_codes[:, unit(i, g)].bitcast(FP8X4),
                    lhsT_scale=pos_scales[:, unit(i, g)],
                    rhs=ref_codes[c][:, g, :].bitcast(FP4X4),
                    rhs_scale=ref_planes[s][:, g, cols],
                    start=(g == 0),
                    stop=False,
                )

        def mm_site(c, i):
            s, cols = plane_cols(c)
            for g in range(PASSES):
                nc.tensor.matmul_mx(
                    out=bank_of["a", c, i][:],
                    lhsT=neg_codes[:, unit(i, g)].bitcast(FP8X4),
                    lhsT_scale=neg_scales[:, unit(i, g)],
                    rhs=site_codes[c][:, g, :].bitcast(FP8X4),
                    rhs_scale=site_planes[s][SITE_ROW:, g, cols],
                    start=False,
                    stop=(g == PASSES - 1),
                )

        whole = slice(0, BANK)

        def mm_breath_pass(c, i, g, kind="b", cols=whole):
            nc.tensor.matmul_mx(
                out=bank_of[kind, c, i][:, cols],
                lhsT=pos_codes[:, unit(i, g)].bitcast(FP8X4),
                lhsT_scale=pos_scales[:, unit(i, g)],
                rhs=w_codes[c, g][:, cols].bitcast(FP8X4),
                rhs_scale=w_scales[c, g][:, cols],
                start=(g == 0),
                stop=(g == PASSES - 1),
            )

        def mm_breath(c, i, kind="b", cols=whole):
            for g in range(PASSES):
                mm_breath_pass(c, i, g, kind, cols)

        def mm_terminal(c, tiles):
            for i in tiles:
                mm_ref(c, i)
            for i in tiles:
                mm_site(c, i)

        def park(c, i, cols=whole, copy=nc.scalar.copy):
            copy(out=result[c, i][:, cols], in_=bank_of["a", c, i][:, cols])

        def combine(c, i, kind="b", cols=whole):
            nc.vector.scalar_tensor_tensor(
                out=result[c, i][:, cols],
                in0=bank_of[kind, c, i][:, cols],
                scalar=resp_col[:, i : i + 1],
                in1=result[c, i][:, cols],
                op0=ALU.mult,
                op1=ALU.subtract,
            )

        def mm_breath_by_pass(c):
            for g in range(PASSES):
                for i in range(TILES):
                    mm_breath_pass(c, i, g)

        def finish(c, i, cols=whole, engine=nc.vector):
            n = slice(c * BANK + cols.start, c * BANK + cols.stop)
            engine.tensor_tensor(
                out=result[c, i][:, cols], in0=result[c, i][:, cols], in1=gain_all[:, n], op=ALU.mult
            )
            nc.sync.dma_start(out=out_hbm[i][:, n], in_=result[c, i][:, cols])

        sort_words(0)
        sort_words(1)
        sort_words(2)
        for j in range(4):
            turn(j)
        spread_gain(0)
        spread_gain(1)
        quantize_pos(0)
        quantize_pos(1)
        mm_ref(0, 0)
        negate(0)
        quantize_pos(2)
        sort_words(3)
        turn(4)
        turn(5)
        quantize_pos(3)
        quantize_neg(0)
        negate(1)
        quantize_pos(4)
        quantize_neg(1)
        quantize_pos(5)
        negate(2)
        quantize_neg(2)

        for i in range(1, TILES):
            mm_ref(0, i)
        for i in range(TILES):
            mm_site(0, i)
        interleave_scalar(0, 0)
        interleave_scalar(0, 1)
        park(0, 0)
        interleave_scalar(0, 2)
        for i in range(1, TILES):
            park(0, i)
        interleave_vector(0, 0)
        interleave_vector(0, 1)
        quantize_breath(0, 0)
        interleave_vector(0, 2)
        quantize_breath(0, 1)
        quantize_breath(0, 2)
        mm_breath_by_pass(0)

        mm_terminal(1, range(TILES))
        for g in range(PASSES):
            interleave_scalar(1, g)
        interleave_vector(1, 0)
        combine(0, 0)
        interleave_vector(1, 1)
        combine(0, 1)
        quantize_breath(1, 0)
        finish(0, 0)
        combine(0, 2)
        finish(0, 1)
        combine(0, 3)
        quantize_breath(1, 1)
        finish(0, 2)
        interleave_vector(1, 2)
        finish(0, 3)
        quantize_breath(1, 2)
        park(1, 0)
        interleave_scalar(2, 0)
        park(1, 1)
        park(1, 2)
        interleave_scalar(2, 1)
        park(1, 3)
        interleave_scalar(2, 2)
        for i in range(TILES):
            mm_breath(1, i)

        mm_terminal(2, range(3))
        interleave_vector(2, 0)
        interleave_vector(2, 1)
        combine(1, 0)
        quantize_breath(2, 0)
        combine(1, 1)
        finish(1, 0)
        combine(1, 2)
        interleave_vector(2, 2)
        combine(1, 3)
        quantize_breath(2, 1)
        finish(1, 1)
        finish(1, 2)
        quantize_breath(2, 2)
        finish(1, 3)
        for i in range(3):
            park(2, i)
        for i in range(3):
            mm_breath(2, i)
        mm_terminal(2, [3])
        halves = (("b", slice(0, BANK // 2)), ("b2", slice(BANK // 2, BANK)))
        for kind, cols in halves:
            park(2, 3, cols)
        combine(2, 0)
        combine(2, 1)
        finish(2, 0)
        combine(2, 2)
        finish(2, 1)
        finish(2, 2)
        for kind, cols in halves:
            mm_breath(2, 3, kind, cols)
            combine(2, 3, kind, cols)
        for kind, cols in halves:
            finish(2, 3, cols)
